import numpy as np
import ml_dtypes


def mxq(x, axis, fmt="e4m3"):
    dtype, down = {"e4m3": (ml_dtypes.float8_e4m3fn, 7), "e5m2": (ml_dtypes.float8_e5m2, 14)}[fmt]
    v = np.moveaxis(np.asarray(x, np.float32).astype(ml_dtypes.bfloat16).astype(np.float64), axis, -1)
    blocks = v.reshape(v.shape[:-1] + (-1, 32))
    amax = np.abs(blocks).max(-1, keepdims=True)
    byte = np.maximum(np.where(amax > 0, np.frexp(amax)[1] - 1 + 127, 0) - down, 1)
    scale = np.exp2(byte - 127.0)
    codes = (blocks / scale).astype(np.float32).astype(dtype).astype(np.float64)
    return np.moveaxis((codes * scale).reshape(v.shape), -1, axis)


WIDE = False


def mx_kscale(k):
    if not WIDE:
        return np.ones(k)
    levels = np.array([10, -10, 5, -5, 0])
    if k % 512:
        return np.exp2(np.random.permutation(np.resize(levels, k // 32))).repeat(32)
    a = np.empty((k // 512, 16))
    for p in range(k // 512):
        a[p, :8] = np.random.permutation(np.resize(levels, 8))
        for g in range(8):
            far = levels[np.abs(levels - a[p, g]) >= 10]
            a[p, g + 8] = far[np.random.randint(len(far))]
    return np.exp2(a.ravel()).repeat(32)


def f64(x):
    return np.asarray(x).astype(np.float64)


def striped(idx):
    return np.tile(idx.reshape(-1, 16).T, (8, 1)).astype(np.uint16)


def unstriped(offs):
    return offs[:16].T.reshape(-1).astype(np.int64)


def striped8(idx):
    return np.concatenate([x.reshape(-1, 16).T for x in idx]).astype(np.uint16)


def runs(offs, k):
    lists = np.stack([offs[16 * r : 16 * r + 16].T.reshape(-1) for r in range(8)]).astype(np.int64)
    return lists[np.arange(k) % 512 // 64]


def pack_weight(w):
    k, n = w.shape
    w = f64(np.asarray(w, np.float32).astype(ml_dtypes.bfloat16)).reshape(k // 32, 32, n)
    amax = np.abs(w).max(1)
    byte = np.clip(np.where(amax > 0, np.frexp(amax)[1] - 1 + 127 - 7, 1), 1, 254)
    scaled = (w * np.exp2(127.0 - byte)[:, None, :]).reshape(k, n).astype(np.float32)
    words = np.ascontiguousarray(scaled.reshape(k // 512, 128, 4, n).transpose(0, 1, 3, 2)).astype(ml_dtypes.float8_e4m3fn).view(np.uint8)
    return words, np.ascontiguousarray(byte.astype(np.uint8).reshape(k // 512, 16, n))


def unpack_weight(words, scales):
    g, p, n, _ = words.shape
    vals = np.ascontiguousarray(words).view(ml_dtypes.float8_e4m3fn).astype(np.float64) * np.repeat(np.exp2(scales.astype(np.float64) - 127.0), 8, axis=1)[..., None]
    return vals.transpose(0, 1, 3, 2).reshape(g * 512, n)


K, T, S, N, G, H, J = 512, 2048, 512, 512, 2048, 512, 512


def setup_inputs():
    n = np.random.standard_normal
    s = mx_kscale(K)[:, None]
    u = mx_kscale(S)
    packed_xT = pack_weight(n((K, T)) * s)
    packed_dT = pack_weight(n((K, G)) / s)
    return {
        "x_words": packed_xT[0],
        "x_scales": packed_xT[1],
        "d_words": packed_dT[0],
        "d_scales": packed_dT[1],
        "gn": (np.random.uniform(0.5, 1.5, (H, 1)) * u[:, None]).astype(np.float32),
        "w1": (n((H, N)) / np.sqrt(H) / u[:, None]).astype(np.float32),
        "tab": n((N, J)).astype(np.float32),
        "offs": striped(np.random.permutation(T)[:S]),
        "kidx": striped8(np.random.randint(0, G, (8, H))),
        "n1": striped8(np.stack([np.random.permutation(S) for _ in range(8)])),
        "n2": striped8(np.stack([np.random.permutation(S) for _ in range(8)])),
        "n3": striped8(np.random.randint(0, J, (8, S))),
        "n4": striped8(np.random.randint(0, J, (8, S))),
        "n5": striped8(np.stack([np.random.permutation(S) for _ in range(8)])),
    }


def reference(x_words, x_scales, d_words, d_scales, gn, w1, tab, offs, kidx, n1, n2, n3, n4, n5):
    d_kidx = unpack_weight(d_words, d_scales)[np.arange(K)[:, None], runs(kidx, K)]
    xq = unpack_weight(x_words, x_scales)[:, unstriped(offs)]
    s = 0.0625 * (d_kidx.T @ xq)
    ex = np.exp(0.5 * s)
    z = f64(gn) * ((2.0 * ex) / (ex + ex[np.arange(H)[:, None], runs(n1, H)] + ex[np.arange(H)[:, None], runs(n2, H)]))
    h = mxq(f64(w1), 0, "e4m3").T @ mxq(z, 0, "e4m3")
    return (h[np.arange(N)[:, None], runs(n5, N)]) * (f64(tab)[np.arange(N)[:, None], runs(n3, N)]) + f64(tab)[np.arange(N)[:, None], runs(n4, N)]

@@ -1,0 +1,190 @@
+from contextlib import ExitStack
+
+import concourse.mybir as mybir
+from concourse.masks import make_identity
+
+K, T, S, N, G, H, J = 512, 2048, 512, 512, 2048, 512, 512
+FLOPS = 2 * K * H * S + 2 * H * N * S
+
+F32 = mybir.dt.float32
+BF16 = mybir.dt.bfloat16
+I32 = mybir.dt.int32
+U32 = mybir.dt.uint32
+U16 = mybir.dt.uint16
+U8 = mybir.dt.uint8
+FP8X4 = mybir.dt.float8_e4m3fn_x4
+ACT = mybir.ActivationFunctionType
+ALU = mybir.AluOpType
+
+P = 128
+PACK = 4
+HALF = 256
+QUART = 128
+LCOLS = 16
+
+
+def tile_picked_keysharekinda_none_p_kernel(
+    tc, x_words, x_scales, d_words, d_scales, gn, w1, tab, offs, kidx, n1, n2, n3, n4, n5, out
+):
+    nc = tc.nc
+    with ExitStack() as ctx:
+        sb = ctx.enter_context(tc.tile_pool(name="sb", bufs=1))
+        ps = ctx.enter_context(tc.psum_pool(name="ps", bufs=1))
+
+        def load_list(src, name):
+            tile = sb.tile([P, S // LCOLS], U16, name=name)
+            nc.sync.dma_start(tile[:], src)
+            return tile
+
+        def part(lst, start, count):
+            return lst[:, start // LCOLS : (start + count) // LCOLS]
+
+        def load_scale_rows(src, name, tag):
+            tile = sb.tile([P, T], U8, name=name, align_bytes=64, tag=tag)
+            nc.sync.dma_start(tile[:].bitcast(I32), src[0].bitcast(I32).unsqueeze(1).to_broadcast([16, 8, T // 4]))
+            return tile
+
+        def load_words(src, name, tag):
+            tile = sb.tile([P, T], U32, name=name, align_bytes=64, tag=tag)
+            nc.sync.dma_start(tile[:].bitcast(I32), src[0].rearrange("p n t -> p (n t)").bitcast(I32))
+            return tile
+
+        kidx_t = load_list(kidx, "kidx_t")
+        dsc_win = load_scale_rows(d_scales, "dsc_win", "dsc_win")
+        offs_t = load_list(offs, "offs_t")
+        xsc_win = load_scale_rows(x_scales, "xsc_win", "xsc_win")
+        dw_win = load_words(d_words, "dw_win", "late0")
+        n1_t = load_list(n1, "n1_t")
+        n2_t = load_list(n2, "n2_t")
+        n3_t = load_list(n3, "n3_t")
+        xw_win = load_words(x_words, "xw_win", "late4")
+        n4_t = load_list(n4, "n4_t")
+        n5_t = load_list(n5, "n5_t")
+
+        planes = sb.tile([P, H + S], U8, align_bytes=64, tag="late5")
+        dsc_pick = sb.tile([P, H], U8, align_bytes=64)
+        nc.vector.tensor_copy(dsc_pick[:], dsc_win[:].indirect(kidx_t[:]))
+        xsc_pick = sb.tile([P, S], U8, align_bytes=64)
+        nc.vector.tensor_copy(xsc_pick[:], xsc_win[:].indirect(offs_t[:]))
+        nc.vector.tensor_copy(
+            planes[:, 0:H].rearrange("p (t m) -> p m t", t=PACK), dsc_pick[:].rearrange("p (m t) -> p m t", t=PACK)
+        )
+        nc.vector.tensor_copy(planes[:, H : H + S].bitcast(I32), xsc_pick[:].bitcast(I32))
+        for r in range(1, 4):
+            nc.scalar.dma_start(planes[r:P:32, :].bitcast(I32), planes[8 * r : P : 32, :].bitcast(I32))
+        dw_pick = sb.tile([P, H], U32, align_bytes=64, tag="late1")
+        nc.vector.tensor_copy(dw_pick[:], dw_win[:].indirect(kidx_t[:]))
+        dw = sb.tile([P, PACK, P], U32, align_bytes=64, tag="late2")
+        nc.vector.tensor_copy(dw[:].rearrange("p t m -> p m t"), dw_pick[:].rearrange("p (m t) -> p m t", t=PACK))
+        xw = sb.tile([P, S], U32, align_bytes=64, tag="late3")
+        nc.vector.tensor_copy(xw[:], xw_win[:].indirect(offs_t[:]))
+
+        ident = sb.tile([P, P], F32)
+        make_identity(nc, ident[:])
+
+        s_ps = []
+        a_t = []
+        for t in range(PACK):
+            bank = ps.tile([P, S], F32, name="s_ps%d" % t, tag="bank%d" % t)
+            nc.tensor.matmul_mx(
+                out=bank[:], lhsT=dw[:, t, :].bitcast(FP8X4), lhsT_scale=planes[:, t * P : (t + 1) * P],
+                rhs=xw[:].bitcast(FP8X4), rhs_scale=planes[:, H : H + S], start=True, stop=True,
+            )
+            s_ps.append(bank)
+            a = sb.tile([P, S], F32, name="a%d" % t)
+            nc.scalar.activation(a[:], bank[:], ACT.Exp if t == 0 else ACT.Copy, scale=0.03125)
+            a_t.append(a)
+
+        tab_rows = tab.rearrange("(p t) j -> p t j", t=PACK)
+        tab_t = []
+        for t in range(PACK):
+            tile = sb.tile([P, J], F32, name="tab%d" % t, align_bytes=64, tag="late%d" % t)
+            nc.sync.dma_start(tile[:], tab_rows[:, t, :])
+            tab_t.append(tile)
+        w_raw = sb.tile([P, PACK, N], F32, align_bytes=64, tag="late4")
+        nc.sync.dma_start(w_raw[:], w1.rearrange("(p j) c -> p j c", j=PACK))
+        gn_t = sb.tile([P, PACK], F32, align_bytes=64, tag="late5")
+        nc.sync.dma_start(gn_t[:], gn.rearrange("(p t) o -> p (t o)", t=PACK))
+
+        e1 = sb.tile([P, PACK, S], F32)
+        e2 = sb.tile([P, PACK, S], F32)
+        for j0 in range(0, S, HALF):
+            nc.vector.tensor_copy(e1[:, 0, j0 : j0 + HALF], a_t[0][:].indirect(part(n1_t, j0, HALF)))
+        for j0 in range(0, S, HALF):
+            nc.vector.tensor_tensor(
+                e2[:, 0, j0 : j0 + HALF], a_t[0][:].indirect(part(n2_t, j0, HALF)), e1[:, 0, j0 : j0 + HALF], ALU.add
+            )
+        ut_ps = [ps.tile([P, PACK - 1, P], F32, name="ut_ps%d" % q, tag="bank%d" % (4 + q)) for q in range(4)]
+        for t in range(1, PACK):
+            for j0 in range(0, S, HALF):
+                nc.scalar.activation(e1[:, t, j0 : j0 + HALF], a_t[t][:].indirect(part(n1_t, j0, HALF)), ACT.Exp)
+                nc.scalar.activation(e2[:, t, j0 : j0 + HALF], a_t[t][:].indirect(part(n2_t, j0, HALF)), ACT.Exp)
+                for q in range(j0 // QUART, (j0 + HALF) // QUART):
+                    cols = slice(q * QUART, (q + 1) * QUART)
+                    nc.tensor.matmul(ut_ps[q][:, t - 1, :], e1[:, t, cols], ident[:], start=True, stop=False, is_transpose=True)
+                    nc.tensor.matmul(ut_ps[q][:, t - 1, :], e2[:, t, cols], ident[:], start=False, stop=True, is_transpose=True)
+
+        lg0 = sb.tile([P, S], F32)
+        df = sb.tile([P, PACK, S], F32)
+        nc.scalar.activation(lg0[:], e2[:, 0, :], ACT.Ln)
+        nc.vector.scalar_tensor_tensor(df[:, 0, :], s_ps[0][:], 0.03125, lg0[:], ALU.mult, ALU.subtract)
+        lgt = sb.tile([P, 4, PACK - 1, P], F32)
+        for hf in range(2):
+            for q in (2 * hf, 2 * hf + 1):
+                nc.scalar.activation(lgt[:, q, :, :], ut_ps[q][:], ACT.Ln)
+            for t in range(1, PACK):
+                lg_ps = ps.tile([P, HALF], F32, name="lg_ps%d_%d" % (hf, t), tag="bank%d" % (3 * hf + t))
+                for q in range(2):
+                    nc.tensor.transpose(lg_ps[:, q * QUART : (q + 1) * QUART], lgt[:, 2 * hf + q, t - 1, :], ident[:])
+                cols = slice(hf * HALF, (hf + 1) * HALF)
+                nc.vector.tensor_tensor(df[:, t, cols], a_t[t][:, cols], lg_ps[:], ALU.subtract)
+
+        w_bf = sb.tile([P, PACK, P, PACK], BF16, align_bytes=64)
+        nc.vector.tensor_copy(w_bf[:].rearrange("p t m j -> p m t j"), w_raw[:].rearrange("p j (m t) -> p m t j", t=PACK))
+        w_codes = sb.tile([P, N], U32, align_bytes=64)
+        w_sc = sb.tile([P, N], U8, align_bytes=64)
+        nc.vector.quantize_mx(out=w_codes[:].bitcast(FP8X4), scales=w_sc[:], in_=w_bf[:].rearrange("p t m j -> p (t m j)"))
+        gn2 = sb.tile([P, PACK], F32)
+        nc.vector.tensor_scalar(gn2[:], gn_t[:], 2.0, None, ALU.mult)
+
+        h_t = [sb.tile([P, S], F32, name="h%d" % t) for t in range(PACK)]
+        h_ps = []
+        sg = sb.tile([P, PACK, S], F32)
+        for j0 in range(0, S, QUART):
+            nc.scalar.activation(sg[:, :, j0 : j0 + QUART], df[:, :, j0 : j0 + QUART], ACT.Sigmoid)
+            z_bf = sb.tile([P, QUART, PACK], BF16, name="z_bf%d" % j0, align_bytes=64)
+            nc.vector.tensor_tensor(
+                z_bf[:].rearrange("p (c i) t -> p c t i", i=4),
+                sg[:, :, j0 : j0 + QUART].rearrange("p t (c i) -> p c t i", i=4),
+                gn2[:].unsqueeze(1).unsqueeze(3).to_broadcast([P, QUART // 4, PACK, 4]),
+                ALU.mult,
+            )
+            z_codes = sb.tile([P, QUART], U32, name="z_codes%d" % j0, align_bytes=64)
+            z_sc = sb.tile([P, QUART], U8, name="z_sc%d" % j0, align_bytes=64)
+            nc.vector.quantize_mx(out=z_codes[:].bitcast(FP8X4), scales=z_sc[:], in_=z_bf[:].rearrange("p j t -> p (j t)"))
+            bank = ps.tile([P, PACK, QUART], F32, name="h_ps%d" % j0, tag="bank%d" % (j0 // QUART))
+            for t in range(PACK):
+                nc.tensor.matmul_mx(
+                    out=bank[:, t, :], lhsT=w_codes[:, t * P : (t + 1) * P].bitcast(FP8X4), lhsT_scale=w_sc[:, t * P : (t + 1) * P],
+                    rhs=z_codes[:].bitcast(FP8X4), rhs_scale=z_sc[:], start=True, stop=True,
+                )
+            h_ps.append(bank)
+        for t in range(PACK):
+            for q in range(S // QUART):
+                nc.scalar.copy(h_t[t][:, q * QUART : (q + 1) * QUART], h_ps[q][:, t, :])
+
+        g3 = sb.tile([P, PACK, S], F32)
+        g4 = sb.tile([P, PACK, S], F32)
+        for t in range(PACK):
+            for j0 in range(0, S, HALF):
+                nc.vector.tensor_copy(g3[:, t, j0 : j0 + HALF], tab_t[t][:].indirect(part(n3_t, j0, HALF)))
+                nc.vector.tensor_copy(g4[:, t, j0 : j0 + HALF], tab_t[t][:].indirect(part(n4_t, j0, HALF)))
+
+        out_rows = out.rearrange("(p t) j -> p t j", t=PACK)
+        y = sb.tile([P, PACK, S], F32)
+        res = sb.tile([P, PACK, S], F32)
+        for t in range(PACK):
+            for j0 in range(0, S, HALF):
+                nc.vector.tensor_tensor(y[:, t, j0 : j0 + HALF], h_t[t][:].indirect(part(n5_t, j0, HALF)), g3[:, t, j0 : j0 + HALF], ALU.mult)
+            nc.vector.tensor_tensor(res[:, t, :], y[:, t, :], g4[:, t, :], ALU.add)
+            nc.sync.dma_start(out_rows[:, t, :], res[:, t, :])

@@ -21,6 +21,7 @@ PACK = 4
 HALF = 256
 QUART = 128
 LCOLS = 16
+VV = [0]
 
 
 def tile_picked_keysharekinda_none_p_kernel(
@@ -36,28 +37,28 @@ def tile_picked_keysharekinda_none_p_kernel(
             nc.sync.dma_start(tile[:], src)
             return tile
 
-        def part(lst, start, count):
-            return lst[:, start // LCOLS : (start + count) // LCOLS]
-
-        def load_scale_rows(src, name, tag):
-            tile = sb.tile([P, T], U8, name=name, align_bytes=64, tag=tag)
-            nc.sync.dma_start(tile[:].bitcast(I32), src[0].bitcast(I32).unsqueeze(1).to_broadcast([16, 8, T // 4]))
-            return tile
-
         def load_words(src, name, tag):
             tile = sb.tile([P, T], U32, name=name, align_bytes=64, tag=tag)
             nc.sync.dma_start(tile[:].bitcast(I32), src[0].rearrange("p n t -> p (n t)").bitcast(I32))
             return tile
 
+        def load_scale_rows(src, name):
+            tile = sb.tile([P, T], U8, name=name, align_bytes=64)
+            nc.sync.dma_start(tile[:].bitcast(I32), src[0].bitcast(I32).unsqueeze(1).to_broadcast([16, 8, T // 4]))
+            return tile
+
         kidx_t = load_list(kidx, "kidx_t")
-        dsc_win = load_scale_rows(d_scales, "dsc_win", "dsc_win")
+        dsc_win = load_scale_rows(d_scales, "dsc_win")
         offs_t = load_list(offs, "offs_t")
-        xsc_win = load_scale_rows(x_scales, "xsc_win", "xsc_win")
+        xsc_win = load_scale_rows(x_scales, "xsc_win")
         dw_win = load_words(d_words, "dw_win", "late0")
         n1_t = load_list(n1, "n1_t")
         n2_t = load_list(n2, "n2_t")
         n3_t = load_list(n3, "n3_t")
         xw_win = load_words(x_words, "xw_win", "late4")
+        tab_rows = tab.rearrange("(p t) j -> p t j", t=PACK)
+        tab0 = sb.tile([P, 2 * J], F32, align_bytes=64)
+        nc.sync.dma_start(tab0[:, 0:J], tab_rows[:, 0, :])
         n4_t = load_list(n4, "n4_t")
         n5_t = load_list(n5, "n5_t")
 
@@ -67,7 +68,8 @@ def tile_picked_keysharekinda_none_p_kernel(
         xsc_pick = sb.tile([P, S], U8, align_bytes=64)
         nc.vector.tensor_copy(xsc_pick[:], xsc_win[:].indirect(offs_t[:]))
         nc.vector.tensor_copy(
-            planes[:, 0:H].rearrange("p (t m) -> p m t", t=PACK), dsc_pick[:].rearrange("p (m t) -> p m t", t=PACK)
+            planes[:, 0:H].bitcast(I32).rearrange("p (t b r) -> p t b r", t=PACK, r=2),
+            dsc_pick[:].bitcast(I32).rearrange("p (b t r) -> p t b r", t=PACK, r=2),
         )
         nc.vector.tensor_copy(planes[:, H : H + S].bitcast(I32), xsc_pick[:].bitcast(I32))
         for r in range(1, 4):
@@ -75,60 +77,66 @@ def tile_picked_keysharekinda_none_p_kernel(
         dw_pick = sb.tile([P, H], U32, align_bytes=64, tag="late1")
         nc.vector.tensor_copy(dw_pick[:], dw_win[:].indirect(kidx_t[:]))
         dw = sb.tile([P, PACK, P], U32, align_bytes=64, tag="late2")
-        nc.vector.tensor_copy(dw[:].rearrange("p t m -> p m t"), dw_pick[:].rearrange("p (m t) -> p m t", t=PACK))
+        nc.vector.tensor_copy(dw[:].rearrange("p t (b r) -> p t b r", r=8), dw_pick[:].rearrange("p (b t r) -> p t b r", t=PACK, r=8))
         xw = sb.tile([P, S], U32, align_bytes=64, tag="late3")
-        nc.vector.tensor_copy(xw[:], xw_win[:].indirect(offs_t[:]))
+        for j0 in range(0, S, HALF):
+            nc.vector.tensor_copy(xw[:, j0 : j0 + HALF], xw_win[:].indirect(offs_t[:, j0 // LCOLS : (j0 + HALF) // LCOLS]))
 
         ident = sb.tile([P, P], F32)
         make_identity(nc, ident[:])
 
-        s_ps = []
+        s_ps = [ps.tile([P, S], F32, name="s_ps%d" % t, tag="bank%d" % t) for t in range(PACK)]
+        for pair in range(0, PACK, 2):
+            for j0 in range(0, S, HALF):
+                for t in (pair, pair + 1):
+                    nc.tensor.matmul_mx(
+                        out=s_ps[t][:, j0 : j0 + HALF], lhsT=dw[:, t, :].bitcast(FP8X4), lhsT_scale=planes[:, t * P : (t + 1) * P],
+                        rhs=xw[:, j0 : j0 + HALF].bitcast(FP8X4), rhs_scale=planes[:, H + j0 : H + j0 + HALF], start=True, stop=True,
+                    )
         a_t = []
         for t in range(PACK):
-            bank = ps.tile([P, S], F32, name="s_ps%d" % t, tag="bank%d" % t)
-            nc.tensor.matmul_mx(
-                out=bank[:], lhsT=dw[:, t, :].bitcast(FP8X4), lhsT_scale=planes[:, t * P : (t + 1) * P],
-                rhs=xw[:].bitcast(FP8X4), rhs_scale=planes[:, H : H + S], start=True, stop=True,
-            )
-            s_ps.append(bank)
-            a = sb.tile([P, S], F32, name="a%d" % t)
-            nc.scalar.activation(a[:], bank[:], ACT.Exp if t == 0 else ACT.Copy, scale=0.03125)
+            bank = s_ps[t]
+            a = sb.tile([P, 2 * S], F32, name="a%d" % t)
+            if t in VV:
+                nc.scalar.activation(a[:, 0:S], bank[:], ACT.Exp, scale=0.03125)
+            else:
+                nc.scalar.activation(a[:, 0:S], bank[:], ACT.Copy, scale=0.03125)
             a_t.append(a)
 
-        tab_rows = tab.rearrange("(p t) j -> p t j", t=PACK)
-        tab_t = []
-        for t in range(PACK):
-            tile = sb.tile([P, J], F32, name="tab%d" % t, align_bytes=64, tag="late%d" % t)
-            nc.sync.dma_start(tile[:], tab_rows[:, t, :])
+        tab_t = [tab0]
+        for t in range(1, PACK):
+            tile = sb.tile([P, 2 * J], F32, name="tab%d" % t, align_bytes=64, tag="late%d" % (t - 1))
+            nc.sync.dma_start(tile[:, 0:J], tab_rows[:, t, :])
             tab_t.append(tile)
         w_raw = sb.tile([P, PACK, N], F32, align_bytes=64, tag="late4")
-        nc.sync.dma_start(w_raw[:], w1.rearrange("(p j) c -> p j c", j=PACK))
-        gn_t = sb.tile([P, PACK], F32, align_bytes=64, tag="late5")
-        nc.sync.dma_start(gn_t[:], gn.rearrange("(p t) o -> p (t o)", t=PACK))
+        w_rows = w1.rearrange("(b j r) c -> j b r c", j=PACK, r=8)
+        for j in range(PACK):
+            nc.sync.dma_start(w_raw[:, j, :], w_rows[j])
+        gn_t = sb.tile([P, PACK, 8], F32, align_bytes=64, tag="late5")
+        with nc.allow_non_contiguous_dma(reason="one weight a key"):
+            for t in range(PACK):
+                nc.sync.dma_start(gn_t[:, t, 0:1], gn.rearrange("(b t r) o -> t b r o", t=PACK, r=8)[t])
 
         e1 = sb.tile([P, PACK, S], F32)
         e2 = sb.tile([P, PACK, S], F32)
-        for j0 in range(0, S, HALF):
-            nc.vector.tensor_copy(e1[:, 0, j0 : j0 + HALF], a_t[0][:].indirect(part(n1_t, j0, HALF)))
-        for j0 in range(0, S, HALF):
-            nc.vector.tensor_tensor(
-                e2[:, 0, j0 : j0 + HALF], a_t[0][:].indirect(part(n2_t, j0, HALF)), e1[:, 0, j0 : j0 + HALF], ALU.add
-            )
+        u0 = sb.tile([P, S], F32, tag="u0", align_bytes=64)
+        nc.vector.tensor_copy(e1[:, 0, :], a_t[0][:].indirect(n1_t[:]))
+        nc.vector.tensor_tensor(u0[:], a_t[0][:].indirect(n2_t[:]), e1[:, 0, :], ALU.add)
         ut_ps = [ps.tile([P, PACK - 1, P], F32, name="ut_ps%d" % q, tag="bank%d" % (4 + q)) for q in range(4)]
         for t in range(1, PACK):
-            for j0 in range(0, S, HALF):
-                nc.scalar.activation(e1[:, t, j0 : j0 + HALF], a_t[t][:].indirect(part(n1_t, j0, HALF)), ACT.Exp)
-                nc.scalar.activation(e2[:, t, j0 : j0 + HALF], a_t[t][:].indirect(part(n2_t, j0, HALF)), ACT.Exp)
-                for q in range(j0 // QUART, (j0 + HALF) // QUART):
-                    cols = slice(q * QUART, (q + 1) * QUART)
-                    nc.tensor.matmul(ut_ps[q][:, t - 1, :], e1[:, t, cols], ident[:], start=True, stop=False, is_transpose=True)
-                    nc.tensor.matmul(ut_ps[q][:, t - 1, :], e2[:, t, cols], ident[:], start=False, stop=True, is_transpose=True)
+            for lst, e in ((n1_t, e1), (n2_t, e2)):
+                nc.scalar.activation(e[:, t, :], a_t[t][:].indirect(lst[:]), ACT.Exp)
+                for q in range(4):
+                    nc.tensor.matmul(
+                        ut_ps[q][:, t - 1, :], e[:, t, q * QUART : (q + 1) * QUART], ident[:],
+                        start=(t == 1 and lst is n1_t), stop=(t == PACK - 1 and lst is n2_t), is_transpose=True,
+                    )
 
-        lg0 = sb.tile([P, S], F32)
+        lg0 = sb.tile([P, S], F32, tag="lg0", align_bytes=64)
         df = sb.tile([P, PACK, S], F32)
-        nc.scalar.activation(lg0[:], e2[:, 0, :], ACT.Ln)
+        nc.scalar.activation(lg0[:], u0[:], ACT.Ln)
         nc.vector.scalar_tensor_tensor(df[:, 0, :], s_ps[0][:], 0.03125, lg0[:], ALU.mult, ALU.subtract)
-        lgt = sb.tile([P, 4, PACK - 1, P], F32)
+        lgt = sb.tile([P, 4, PACK - 1, P], F32, tag="lgt", align_bytes=64)
         for hf in range(2):
             for q in (2 * hf, 2 * hf + 1):
                 nc.scalar.activation(lgt[:, q, :, :], ut_ps[q][:], ACT.Ln)
@@ -145,46 +153,92 @@ def tile_picked_keysharekinda_none_p_kernel(
         w_sc = sb.tile([P, N], U8, align_bytes=64)
         nc.vector.quantize_mx(out=w_codes[:].bitcast(FP8X4), scales=w_sc[:], in_=w_bf[:].rearrange("p t m j -> p (t m j)"))
         gn2 = sb.tile([P, PACK], F32)
-        nc.vector.tensor_scalar(gn2[:], gn_t[:], 2.0, None, ALU.mult)
+        nc.vector.tensor_scalar(gn2[:], gn_t[:, :, 0], 2.0, None, ALU.mult)
 
-        h_t = [sb.tile([P, S], F32, name="h%d" % t) for t in range(PACK)]
-        h_ps = []
+        h_t = [sb.tile([P, 2 * S], F32, name="h%d" % t) for t in range(PACK)]
+        h_ps = [ps.tile([P, S], F32, name="h_ps%d" % t, tag="bank%d" % t) for t in range(PACK)]
         sg = sb.tile([P, PACK, S], F32)
-        for j0 in range(0, S, QUART):
-            nc.scalar.activation(sg[:, :, j0 : j0 + QUART], df[:, :, j0 : j0 + QUART], ACT.Sigmoid)
-            z_bf = sb.tile([P, QUART, PACK], BF16, name="z_bf%d" % j0, align_bytes=64)
+
+        z_codes = sb.tile([P, S], U32, align_bytes=64)
+        z_sc = sb.tile([P, S], U8, align_bytes=64)
+
+        def second_product(t, j0, wd):
+            nc.tensor.matmul_mx(
+                out=h_ps[t][:, j0 : j0 + wd],
+                lhsT=w_codes[:, t * P : (t + 1) * P].bitcast(FP8X4), lhsT_scale=w_sc[:, t * P : (t + 1) * P],
+                rhs=z_codes[:, j0 : j0 + wd].bitcast(FP8X4), rhs_scale=z_sc[:, j0 : j0 + wd], start=True, stop=True,
+            )
+
+        def weigh(z_bf, j0, lo, wd):
+            nc.scalar.activation(sg[:, :, j0 + lo : j0 + lo + wd], df[:, :, j0 + lo : j0 + lo + wd], ACT.Sigmoid)
             nc.vector.tensor_tensor(
-                z_bf[:].rearrange("p (c i) t -> p c t i", i=4),
-                sg[:, :, j0 : j0 + QUART].rearrange("p t (c i) -> p c t i", i=4),
-                gn2[:].unsqueeze(1).unsqueeze(3).to_broadcast([P, QUART // 4, PACK, 4]),
+                z_bf[:, lo : lo + wd, :].rearrange("p (c i) t -> p c t i", i=4),
+                sg[:, :, j0 + lo : j0 + lo + wd].rearrange("p t (c i) -> p c t i", i=4),
+                gn2[:].unsqueeze(1).unsqueeze(3).to_broadcast([P, wd // 4, PACK, 4]),
                 ALU.mult,
             )
-            z_codes = sb.tile([P, QUART], U32, name="z_codes%d" % j0, align_bytes=64)
-            z_sc = sb.tile([P, QUART], U8, name="z_sc%d" % j0, align_bytes=64)
-            nc.vector.quantize_mx(out=z_codes[:].bitcast(FP8X4), scales=z_sc[:], in_=z_bf[:].rearrange("p j t -> p (j t)"))
-            bank = ps.tile([P, PACK, QUART], F32, name="h_ps%d" % j0, tag="bank%d" % (j0 // QUART))
-            for t in range(PACK):
-                nc.tensor.matmul_mx(
-                    out=bank[:, t, :], lhsT=w_codes[:, t * P : (t + 1) * P].bitcast(FP8X4), lhsT_scale=w_sc[:, t * P : (t + 1) * P],
-                    rhs=z_codes[:].bitcast(FP8X4), rhs_scale=z_sc[:], start=True, stop=True,
-                )
-            h_ps.append(bank)
-        for t in range(PACK):
-            for q in range(S // QUART):
-                nc.scalar.copy(h_t[t][:, q * QUART : (q + 1) * QUART], h_ps[q][:, t, :])
 
-        g3 = sb.tile([P, PACK, S], F32)
-        g4 = sb.tile([P, PACK, S], F32)
+        def quantise(z_bf, j0, wd):
+            nc.vector.quantize_mx(
+                out=z_codes[:, j0 : j0 + wd].bitcast(FP8X4), scales=z_sc[:, j0 : j0 + wd], in_=z_bf[:].rearrange("p j t -> p (j t)")
+            )
+
+        pending = None
+        for j0, wd in ((0, 128), (128, 128), (256, 128), (384, 64), (448, 64)):
+            z_bf = sb.tile([P, wd, PACK], BF16, name="z_bf%d" % j0, tag="z_bf%d" % j0, align_bytes=64)
+            if j0 == 0:
+                weigh(z_bf, j0, 0, 64)
+                weigh(z_bf, j0, 64, 64)
+            else:
+                weigh(z_bf, j0, 0, wd)
+            if pending is not None:
+                quantise(*pending)
+            pending = (z_bf, j0, wd)
+        quantise(*pending)
+        for j0 in range(0, S, HALF):
+            for t in range(PACK):
+                second_product(t, j0, HALF)
+                nc.scalar.copy(h_t[t][:, j0 : j0 + HALF], h_ps[t][:, j0 : j0 + HALF])
+
+        g3 = []
+        g4 = []
         for t in range(PACK):
-            for j0 in range(0, S, HALF):
-                nc.vector.tensor_copy(g3[:, t, j0 : j0 + HALF], tab_t[t][:].indirect(part(n3_t, j0, HALF)))
-                nc.vector.tensor_copy(g4[:, t, j0 : j0 + HALF], tab_t[t][:].indirect(part(n4_t, j0, HALF)))
+            g3.append(sb.tile([P, S], F32, name="g3_%d" % t))
+            nc.vector.tensor_copy(g3[t][:], tab_t[t][:].indirect(n3_t[:]))
+            if t < PACK - 1:
+                g4.append(sb.tile([P, S], F32, name="g4_%d" % t))
+                nc.vector.tensor_copy(g4[t][:], tab_t[t][:].indirect(n4_t[:]))
+        g4_last = []
+        for j0, tag in ((0, "lgt"), (HALF, "z_bf448")):
+            tile = sb.tile([P, HALF], F32, name="g4_last%d" % j0, tag=tag, align_bytes=64)
+            nc.vector.tensor_copy(tile[:], tab_t[PACK - 1][:].indirect(n4_t[:, j0 // LCOLS : (j0 + HALF) // LCOLS]))
+            g4_last.append(tile)
 
         out_rows = out.rearrange("(p t) j -> p t j", t=PACK)
         y = sb.tile([P, PACK, S], F32)
         res = sb.tile([P, PACK, S], F32)
         for t in range(PACK):
-            for j0 in range(0, S, HALF):
-                nc.vector.tensor_tensor(y[:, t, j0 : j0 + HALF], h_t[t][:].indirect(part(n5_t, j0, HALF)), g3[:, t, j0 : j0 + HALF], ALU.mult)
-            nc.vector.tensor_tensor(res[:, t, :], y[:, t, :], g4[:, t, :], ALU.add)
-            nc.sync.dma_start(out_rows[:, t, :], res[:, t, :])
+            nc.vector.tensor_tensor(y[:, t, :], h_t[t][:].indirect(n5_t[:]), g3[t][:], ALU.mult)
+            if t < 1:
+                sum_ps = ps.tile([P, 4, P], F32, name="sum_ps%d" % t, tag="bank4")
+                for first, src in ((True, g4[t][:]), (False, y[:, t, :])):
+                    for q in range(4):
+                        nc.tensor.matmul(
+                            sum_ps[:, q, :], src[:, q * QUART : (q + 1) * QUART], ident[:],
+                            start=(first and q == 0), stop=(not first and q == 3), is_transpose=True,
+                        )
+                sum_t = sb.tile([P, 4, P], F32, name="sum_t%d" % t)
+                nc.scalar.copy(sum_t[:], sum_ps[:])
+                back_ps = ps.tile([P, S], F32, name="back_ps%d" % t, tag="bank%d" % (5 + t))
+                for q in range(4):
+                    nc.tensor.transpose(back_ps[:, q * QUART : (q + 1) * QUART], sum_t[:, q, :], ident[:])
+                nc.scalar.copy(res[:, t, :], back_ps[:])
+                nc.scalar.dma_start(out_rows[:, t, :], res[:, t, :])
+            elif t < PACK - 1:
+                nc.vector.tensor_tensor(res[:, t, :], y[:, t, :], g4[t][:], ALU.add)
+                nc.sync.dma_start(out_rows[:, t, :], res[:, t, :])
+            else:
+                for hf in range(2):
+                    cols = slice(hf * HALF, (hf + 1) * HALF)
+                    nc.vector.tensor_tensor(res[:, t, cols], y[:, t, cols], g4_last[hf][:], ALU.add)
+                    nc.sync.dma_start(out_rows[:, t, cols], res[:, t, cols])

@@ -148,7 +148,7 @@ def tile_picked_keysharekinda_none_p_kernel(
                 nc.vector.tensor_tensor(df[:, t, cols], a_t[t][:, cols], lg_ps[:], ALU.subtract)
 
         w_bf = sb.tile([P, PACK, P, PACK], BF16, align_bytes=64)
-        nc.vector.tensor_copy(w_bf[:].rearrange("p t m j -> p m t j"), w_raw[:].rearrange("p j (m t) -> p m t j", t=PACK))
+        nc.gpsimd.tensor_scalar(w_bf[:].rearrange("p t m j -> p m t j"), w_raw[:].rearrange("p j (m t) -> p m t j", t=PACK), 1.0, 0.0, ALU.mult, ALU.add)
         w_codes = sb.tile([P, N], U32, align_bytes=64)
         w_sc = sb.tile([P, N], U8, align_bytes=64)
         nc.vector.quantize_mx(out=w_codes[:].bitcast(FP8X4), scales=w_sc[:], in_=w_bf[:].rearrange("p t m j -> p (t m j)"))

@@ -5,6 +5,7 @@ from concourse.masks import make_identity
 
 K, T, S, N, G, H, J = 512, 2048, 512, 512, 2048, 512, 512
 FLOPS = 2 * K * H * S + 2 * H * N * S
+assert T == G
 
 F32 = mybir.dt.float32
 BF16 = mybir.dt.bfloat16
@@ -18,10 +19,14 @@ ALU = mybir.AluOpType
 
 P = 128
 PACK = 4
-HALF = 256
-QUART = 128
+HALF = S // 2
+QUART = S // 4
 LCOLS = 16
-VV = [0]
+RUN = 8
+SCALE_ROWS = K // 32
+HALF_SCORE = 0.5 * 0.0625
+Z_PIECES = ((0, 128), (128, 128), (256, 128), (384, 64), (448, 64))
+FIRST_STEP = 64
 
 
 def tile_picked_keysharekinda_none_p_kernel(
@@ -37,6 +42,9 @@ def tile_picked_keysharekinda_none_p_kernel(
             nc.sync.dma_start(tile[:], src)
             return tile
 
+        def entries(lst, first, count):
+            return lst[:, first // LCOLS : (first + count) // LCOLS]
+
         def load_words(src, name, tag):
             tile = sb.tile([P, T], U32, name=name, align_bytes=64, tag=tag)
             nc.sync.dma_start(tile[:].bitcast(I32), src[0].rearrange("p n t -> p (n t)").bitcast(I32))
@@ -44,7 +52,9 @@ def tile_picked_keysharekinda_none_p_kernel(
 
         def load_scale_rows(src, name):
             tile = sb.tile([P, T], U8, name=name, align_bytes=64)
-            nc.sync.dma_start(tile[:].bitcast(I32), src[0].bitcast(I32).unsqueeze(1).to_broadcast([16, 8, T // 4]))
+            nc.sync.dma_start(
+                tile[:].bitcast(I32), src[0].bitcast(I32).unsqueeze(1).to_broadcast([SCALE_ROWS, RUN, T // 4])
+            )
             return tile
 
         kidx_t = load_list(kidx, "kidx_t")
@@ -68,19 +78,21 @@ def tile_picked_keysharekinda_none_p_kernel(
         xsc_pick = sb.tile([P, S], U8, align_bytes=64)
         nc.vector.tensor_copy(xsc_pick[:], xsc_win[:].indirect(offs_t[:]))
         nc.vector.tensor_copy(
-            planes[:, 0:H].bitcast(I32).rearrange("p (t b r) -> p t b r", t=PACK, r=2),
-            dsc_pick[:].bitcast(I32).rearrange("p (b t r) -> p t b r", t=PACK, r=2),
+            planes[:, 0:H].bitcast(I32).rearrange("p (t b r) -> p t b r", t=PACK, r=RUN // 4),
+            dsc_pick[:].bitcast(I32).rearrange("p (b t r) -> p t b r", t=PACK, r=RUN // 4),
         )
         nc.vector.tensor_copy(planes[:, H : H + S].bitcast(I32), xsc_pick[:].bitcast(I32))
         for r in range(1, 4):
-            nc.scalar.dma_start(planes[r:P:32, :].bitcast(I32), planes[8 * r : P : 32, :].bitcast(I32))
+            nc.scalar.dma_start(planes[r:P:32, :].bitcast(I32), planes[RUN * r : P : 32, :].bitcast(I32))
         dw_pick = sb.tile([P, H], U32, align_bytes=64, tag="late1")
         nc.vector.tensor_copy(dw_pick[:], dw_win[:].indirect(kidx_t[:]))
         dw = sb.tile([P, PACK, P], U32, align_bytes=64, tag="late2")
-        nc.vector.tensor_copy(dw[:].rearrange("p t (b r) -> p t b r", r=8), dw_pick[:].rearrange("p (b t r) -> p t b r", t=PACK, r=8))
-        xw = sb.tile([P, S], U32, align_bytes=64, tag="late3")
+        nc.vector.tensor_copy(
+            dw[:].rearrange("p t (b r) -> p t b r", r=RUN), dw_pick[:].rearrange("p (b t r) -> p t b r", t=PACK, r=RUN)
+        )
+        xw = sb.tile([P, S], U32, align_bytes=64)
         for j0 in range(0, S, HALF):
-            nc.vector.tensor_copy(xw[:, j0 : j0 + HALF], xw_win[:].indirect(offs_t[:, j0 // LCOLS : (j0 + HALF) // LCOLS]))
+            nc.vector.tensor_copy(xw[:, j0 : j0 + HALF], xw_win[:].indirect(entries(offs_t, j0, HALF)))
 
         ident = sb.tile([P, P], F32)
         make_identity(nc, ident[:])
@@ -90,17 +102,23 @@ def tile_picked_keysharekinda_none_p_kernel(
             for j0 in range(0, S, HALF):
                 for t in (pair, pair + 1):
                     nc.tensor.matmul_mx(
-                        out=s_ps[t][:, j0 : j0 + HALF], lhsT=dw[:, t, :].bitcast(FP8X4), lhsT_scale=planes[:, t * P : (t + 1) * P],
-                        rhs=xw[:, j0 : j0 + HALF].bitcast(FP8X4), rhs_scale=planes[:, H + j0 : H + j0 + HALF], start=True, stop=True,
+                        out=s_ps[t][:, j0 : j0 + HALF],
+                        lhsT=dw[:, t, :].bitcast(FP8X4),
+                        lhsT_scale=planes[:, t * P : (t + 1) * P],
+                        rhs=xw[:, j0 : j0 + HALF].bitcast(FP8X4),
+                        rhs_scale=planes[:, H + j0 : H + j0 + HALF],
+                        start=True,
+                        stop=True,
                     )
         a_t = []
         for t in range(PACK):
-            bank = s_ps[t]
             a = sb.tile([P, 2 * S], F32, name="a%d" % t)
-            if t in VV:
-                nc.scalar.activation(a[:, 0:S], bank[:], ACT.Exp, scale=0.03125)
+            if t == 0:
+                nc.scalar.activation(a[:, 0:S], s_ps[t][:], ACT.Exp, scale=HALF_SCORE)
+            elif t < PACK - 1:
+                nc.scalar.activation(a[:, 0:S], s_ps[t][:], ACT.Copy, scale=HALF_SCORE)
             else:
-                nc.scalar.activation(a[:, 0:S], bank[:], ACT.Copy, scale=0.03125)
+                nc.vector.tensor_scalar(a[:, 0:S], s_ps[t][:], HALF_SCORE, None, ALU.mult)
             a_t.append(a)
 
         tab_t = [tab0]
@@ -109,46 +127,57 @@ def tile_picked_keysharekinda_none_p_kernel(
             nc.sync.dma_start(tile[:, 0:J], tab_rows[:, t, :])
             tab_t.append(tile)
         w_raw = sb.tile([P, PACK, N], F32, align_bytes=64, tag="late4")
-        w_rows = w1.rearrange("(b j r) c -> j b r c", j=PACK, r=8)
+        w_rows = w1.rearrange("(b j r) c -> j b r c", j=PACK, r=RUN)
         for j in range(PACK):
             nc.sync.dma_start(w_raw[:, j, :], w_rows[j])
         gn_t = sb.tile([P, PACK, 8], F32, align_bytes=64, tag="late5")
         with nc.allow_non_contiguous_dma(reason="one weight a key"):
             for t in range(PACK):
-                nc.sync.dma_start(gn_t[:, t, 0:1], gn.rearrange("(b t r) o -> t b r o", t=PACK, r=8)[t])
+                nc.sync.dma_start(gn_t[:, t, 0:1], gn.rearrange("(b t r) o -> t b r o", t=PACK, r=RUN)[t])
 
         e1 = sb.tile([P, PACK, S], F32)
         e2 = sb.tile([P, PACK, S], F32)
-        u0 = sb.tile([P, S], F32, tag="u0", align_bytes=64)
+        u0 = sb.tile([P, S], F32, align_bytes=64)
         nc.vector.tensor_copy(e1[:, 0, :], a_t[0][:].indirect(n1_t[:]))
         nc.vector.tensor_tensor(u0[:], a_t[0][:].indirect(n2_t[:]), e1[:, 0, :], ALU.add)
-        ut_ps = [ps.tile([P, PACK - 1, P], F32, name="ut_ps%d" % q, tag="bank%d" % (4 + q)) for q in range(4)]
+        ut_ps = [ps.tile([P, PACK - 1, P], F32, name="ut_ps%d" % q, tag="bank%d" % (PACK + q)) for q in range(S // QUART)]
         for t in range(1, PACK):
             for lst, e in ((n1_t, e1), (n2_t, e2)):
                 nc.scalar.activation(e[:, t, :], a_t[t][:].indirect(lst[:]), ACT.Exp)
-                for q in range(4):
+                for q in range(S // QUART):
                     nc.tensor.matmul(
-                        ut_ps[q][:, t - 1, :], e[:, t, q * QUART : (q + 1) * QUART], ident[:],
-                        start=(t == 1 and lst is n1_t), stop=(t == PACK - 1 and lst is n2_t), is_transpose=True,
+                        ut_ps[q][:, t - 1, :],
+                        e[:, t, q * QUART : (q + 1) * QUART],
+                        ident[:],
+                        start=(t == 1 and lst is n1_t),
+                        stop=(t == PACK - 1 and lst is n2_t),
+                        is_transpose=True,
                     )
 
-        lg0 = sb.tile([P, S], F32, tag="lg0", align_bytes=64)
+        lg0 = sb.tile([P, S], F32, align_bytes=64)
         df = sb.tile([P, PACK, S], F32)
         nc.scalar.activation(lg0[:], u0[:], ACT.Ln)
-        nc.vector.scalar_tensor_tensor(df[:, 0, :], s_ps[0][:], 0.03125, lg0[:], ALU.mult, ALU.subtract)
-        lgt = sb.tile([P, 4, PACK - 1, P], F32, tag="lgt", align_bytes=64)
+        nc.vector.scalar_tensor_tensor(df[:, 0, :], s_ps[0][:], HALF_SCORE, lg0[:], ALU.mult, ALU.subtract)
+        lgt = sb.tile([P, S // QUART, PACK - 1, P], F32, tag="lgt", align_bytes=64)
         for hf in range(2):
             for q in (2 * hf, 2 * hf + 1):
                 nc.scalar.activation(lgt[:, q, :, :], ut_ps[q][:], ACT.Ln)
             for t in range(1, PACK):
-                lg_ps = ps.tile([P, HALF], F32, name="lg_ps%d_%d" % (hf, t), tag="bank%d" % (3 * hf + t))
+                lg_ps = ps.tile([P, HALF], F32, name="lg_ps%d_%d" % (hf, t), tag="bank%d" % ((PACK - 1) * hf + t))
                 for q in range(2):
                     nc.tensor.transpose(lg_ps[:, q * QUART : (q + 1) * QUART], lgt[:, 2 * hf + q, t - 1, :], ident[:])
                 cols = slice(hf * HALF, (hf + 1) * HALF)
                 nc.vector.tensor_tensor(df[:, t, cols], a_t[t][:, cols], lg_ps[:], ALU.subtract)
 
         w_bf = sb.tile([P, PACK, P, PACK], BF16, align_bytes=64)
-        nc.gpsimd.tensor_scalar(w_bf[:].rearrange("p t m j -> p m t j"), w_raw[:].rearrange("p j (m t) -> p m t j", t=PACK), 1.0, 0.0, ALU.mult, ALU.add)
+        nc.gpsimd.tensor_scalar(
+            w_bf[:].rearrange("p t m j -> p m t j"),
+            w_raw[:].rearrange("p j (m t) -> p m t j", t=PACK),
+            1.0,
+            0.0,
+            ALU.mult,
+            ALU.add,
+        )
         w_codes = sb.tile([P, N], U32, align_bytes=64)
         w_sc = sb.tile([P, N], U8, align_bytes=64)
         nc.vector.quantize_mx(out=w_codes[:].bitcast(FP8X4), scales=w_sc[:], in_=w_bf[:].rearrange("p t m j -> p (t m j)"))
@@ -158,46 +187,48 @@ def tile_picked_keysharekinda_none_p_kernel(
         h_t = [sb.tile([P, 2 * S], F32, name="h%d" % t) for t in range(PACK)]
         h_ps = [ps.tile([P, S], F32, name="h_ps%d" % t, tag="bank%d" % t) for t in range(PACK)]
         sg = sb.tile([P, PACK, S], F32)
-
         z_codes = sb.tile([P, S], U32, align_bytes=64)
         z_sc = sb.tile([P, S], U8, align_bytes=64)
 
-        def second_product(t, j0, wd):
-            nc.tensor.matmul_mx(
-                out=h_ps[t][:, j0 : j0 + wd],
-                lhsT=w_codes[:, t * P : (t + 1) * P].bitcast(FP8X4), lhsT_scale=w_sc[:, t * P : (t + 1) * P],
-                rhs=z_codes[:, j0 : j0 + wd].bitcast(FP8X4), rhs_scale=z_sc[:, j0 : j0 + wd], start=True, stop=True,
-            )
-
         def weigh(z_bf, j0, lo, wd):
-            nc.scalar.activation(sg[:, :, j0 + lo : j0 + lo + wd], df[:, :, j0 + lo : j0 + lo + wd], ACT.Sigmoid)
+            cols = slice(j0 + lo, j0 + lo + wd)
+            nc.scalar.activation(sg[:, :, cols], df[:, :, cols], ACT.Sigmoid)
             nc.vector.tensor_tensor(
                 z_bf[:, lo : lo + wd, :].rearrange("p (c i) t -> p c t i", i=4),
-                sg[:, :, j0 + lo : j0 + lo + wd].rearrange("p t (c i) -> p c t i", i=4),
+                sg[:, :, cols].rearrange("p t (c i) -> p c t i", i=4),
                 gn2[:].unsqueeze(1).unsqueeze(3).to_broadcast([P, wd // 4, PACK, 4]),
                 ALU.mult,
             )
 
         def quantise(z_bf, j0, wd):
             nc.vector.quantize_mx(
-                out=z_codes[:, j0 : j0 + wd].bitcast(FP8X4), scales=z_sc[:, j0 : j0 + wd], in_=z_bf[:].rearrange("p j t -> p (j t)")
+                out=z_codes[:, j0 : j0 + wd].bitcast(FP8X4),
+                scales=z_sc[:, j0 : j0 + wd],
+                in_=z_bf[:].rearrange("p j t -> p (j t)"),
             )
 
         pending = None
-        for j0, wd in ((0, 128), (128, 128), (256, 128), (384, 64), (448, 64)):
+        for j0, wd in Z_PIECES:
             z_bf = sb.tile([P, wd, PACK], BF16, name="z_bf%d" % j0, tag="z_bf%d" % j0, align_bytes=64)
-            if j0 == 0:
-                weigh(z_bf, j0, 0, 64)
-                weigh(z_bf, j0, 64, 64)
-            else:
-                weigh(z_bf, j0, 0, wd)
+            step = FIRST_STEP if j0 == 0 else wd
+            for lo in range(0, wd, step):
+                weigh(z_bf, j0, lo, step)
             if pending is not None:
                 quantise(*pending)
             pending = (z_bf, j0, wd)
         quantise(*pending)
+
         for j0 in range(0, S, HALF):
             for t in range(PACK):
-                second_product(t, j0, HALF)
+                nc.tensor.matmul_mx(
+                    out=h_ps[t][:, j0 : j0 + HALF],
+                    lhsT=w_codes[:, t * P : (t + 1) * P].bitcast(FP8X4),
+                    lhsT_scale=w_sc[:, t * P : (t + 1) * P],
+                    rhs=z_codes[:, j0 : j0 + HALF].bitcast(FP8X4),
+                    rhs_scale=z_sc[:, j0 : j0 + HALF],
+                    start=True,
+                    stop=True,
+                )
                 nc.scalar.copy(h_t[t][:, j0 : j0 + HALF], h_ps[t][:, j0 : j0 + HALF])
 
         g3 = []
@@ -209,28 +240,39 @@ def tile_picked_keysharekinda_none_p_kernel(
                 g4.append(sb.tile([P, S], F32, name="g4_%d" % t))
                 nc.vector.tensor_copy(g4[t][:], tab_t[t][:].indirect(n4_t[:]))
         g4_last = []
-        for j0, tag in ((0, "lgt"), (HALF, "z_bf448")):
+        for j0, tag in ((0, "lgt"), (HALF, "z_bf%d" % Z_PIECES[-1][0])):
             tile = sb.tile([P, HALF], F32, name="g4_last%d" % j0, tag=tag, align_bytes=64)
-            nc.vector.tensor_copy(tile[:], tab_t[PACK - 1][:].indirect(n4_t[:, j0 // LCOLS : (j0 + HALF) // LCOLS]))
+            nc.vector.tensor_copy(tile[:], tab_t[PACK - 1][:].indirect(entries(n4_t, j0, HALF)))
             g4_last.append(tile)
 
         out_rows = out.rearrange("(p t) j -> p t j", t=PACK)
         y = sb.tile([P, PACK, S], F32)
         res = sb.tile([P, PACK, S], F32)
         for t in range(PACK):
-            nc.vector.tensor_tensor(y[:, t, :], h_t[t][:].indirect(n5_t[:]), g3[t][:], ALU.mult)
-            if t < 1:
-                sum_ps = ps.tile([P, 4, P], F32, name="sum_ps%d" % t, tag="bank4")
+            step = HALF if t == PACK - 1 else S
+            for j0 in range(0, S, step):
+                nc.vector.tensor_tensor(
+                    y[:, t, j0 : j0 + step],
+                    h_t[t][:].indirect(entries(n5_t, j0, step)),
+                    g3[t][:, j0 : j0 + step],
+                    ALU.mult,
+                )
+            if t == 0:
+                sum_ps = ps.tile([P, S // QUART, P], F32, name="sum_ps0", tag="bank4")
                 for first, src in ((True, g4[t][:]), (False, y[:, t, :])):
-                    for q in range(4):
+                    for q in range(S // QUART):
                         nc.tensor.matmul(
-                            sum_ps[:, q, :], src[:, q * QUART : (q + 1) * QUART], ident[:],
-                            start=(first and q == 0), stop=(not first and q == 3), is_transpose=True,
+                            sum_ps[:, q, :],
+                            src[:, q * QUART : (q + 1) * QUART],
+                            ident[:],
+                            start=(first and q == 0),
+                            stop=(not first and q == S // QUART - 1),
+                            is_transpose=True,
                         )
-                sum_t = sb.tile([P, 4, P], F32, name="sum_t%d" % t)
+                sum_t = sb.tile([P, S // QUART, P], F32, name="sum_t0")
                 nc.scalar.copy(sum_t[:], sum_ps[:])
-                back_ps = ps.tile([P, S], F32, name="back_ps%d" % t, tag="bank%d" % (5 + t))
-                for q in range(4):
+                back_ps = ps.tile([P, S], F32, name="back_ps0", tag="bank5")
+                for q in range(S // QUART):
                     nc.tensor.transpose(back_ps[:, q * QUART : (q + 1) * QUART], sum_t[:, q, :], ident[:])
                 nc.scalar.copy(res[:, t, :], back_ps[:])
                 nc.scalar.dma_start(out_rows[:, t, :], res[:, t, :])

from contextlib import ExitStack

import concourse.mybir as mybir
from concourse.masks import make_identity

K, T, S, N, G, H, J = 512, 2048, 512, 512, 2048, 512, 512
FLOPS = 2 * K * H * S + 2 * H * N * S
assert T == G

F32 = mybir.dt.float32
BF16 = mybir.dt.bfloat16
I32 = mybir.dt.int32
U32 = mybir.dt.uint32
U16 = mybir.dt.uint16
U8 = mybir.dt.uint8
FP8X4 = mybir.dt.float8_e4m3fn_x4
ACT = mybir.ActivationFunctionType
ALU = mybir.AluOpType

P = 128
PACK = 4
HALF = S // 2
QUART = S // 4
LCOLS = 16
RUN = 8
SCALE_ROWS = K // 32
HALF_SCORE = 0.5 * 0.0625
Z_PIECES = ((0, 128), (128, 128), (256, 128), (384, 64), (448, 64))
FIRST_STEP = 64


def tile_picked_keysharekinda_none_p_kernel(
    tc, x_words, x_scales, d_words, d_scales, gn, w1, tab, offs, kidx, n1, n2, n3, n4, n5, out
):
    nc = tc.nc
    with ExitStack() as ctx:
        sb = ctx.enter_context(tc.tile_pool(name="sb", bufs=1))
        ps = ctx.enter_context(tc.psum_pool(name="ps", bufs=1))

        def load_list(src, name):
            tile = sb.tile([P, S // LCOLS], U16, name=name)
            nc.sync.dma_start(tile[:], src)
            return tile

        def entries(lst, first, count):
            return lst[:, first // LCOLS : (first + count) // LCOLS]

        def load_words(src, name, tag):
            tile = sb.tile([P, T], U32, name=name, align_bytes=64, tag=tag)
            nc.sync.dma_start(tile[:].bitcast(I32), src[0].rearrange("p n t -> p (n t)").bitcast(I32))
            return tile

        def load_scale_rows(src, name):
            tile = sb.tile([P, T], U8, name=name, align_bytes=64)
            nc.sync.dma_start(
                tile[:].bitcast(I32), src[0].bitcast(I32).unsqueeze(1).to_broadcast([SCALE_ROWS, RUN, T // 4])
            )
            return tile

        kidx_t = load_list(kidx, "kidx_t")
        dsc_win = load_scale_rows(d_scales, "dsc_win")
        offs_t = load_list(offs, "offs_t")
        xsc_win = load_scale_rows(x_scales, "xsc_win")
        dw_win = load_words(d_words, "dw_win", "late0")
        n1_t = load_list(n1, "n1_t")
        n2_t = load_list(n2, "n2_t")
        n3_t = load_list(n3, "n3_t")
        xw_win = load_words(x_words, "xw_win", "late4")
        tab_rows = tab.rearrange("(p t) j -> p t j", t=PACK)
        tab0 = sb.tile([P, 2 * J], F32, align_bytes=64)
        nc.sync.dma_start(tab0[:, 0:J], tab_rows[:, 0, :])
        n4_t = load_list(n4, "n4_t")
        n5_t = load_list(n5, "n5_t")

        planes = sb.tile([P, H + S], U8, align_bytes=64, tag="late5")
        dsc_pick = sb.tile([P, H], U8, align_bytes=64)
        nc.vector.tensor_copy(dsc_pick[:], dsc_win[:].indirect(kidx_t[:]))
        xsc_pick = sb.tile([P, S], U8, align_bytes=64)
        nc.vector.tensor_copy(xsc_pick[:], xsc_win[:].indirect(offs_t[:]))
        nc.vector.tensor_copy(
            planes[:, 0:H].bitcast(I32).rearrange("p (t b r) -> p t b r", t=PACK, r=RUN // 4),
            dsc_pick[:].bitcast(I32).rearrange("p (b t r) -> p t b r", t=PACK, r=RUN // 4),
        )
        nc.vector.tensor_copy(planes[:, H : H + S].bitcast(I32), xsc_pick[:].bitcast(I32))
        for r in range(1, 4):
            nc.scalar.dma_start(planes[r:P:32, :].bitcast(I32), planes[RUN * r : P : 32, :].bitcast(I32))
        dw_pick = sb.tile([P, H], U32, align_bytes=64, tag="late1")
        nc.vector.tensor_copy(dw_pick[:], dw_win[:].indirect(kidx_t[:]))
        dw = sb.tile([P, PACK, P], U32, align_bytes=64, tag="late2")
        nc.vector.tensor_copy(
            dw[:].rearrange("p t (b r) -> p t b r", r=RUN), dw_pick[:].rearrange("p (b t r) -> p t b r", t=PACK, r=RUN)
        )
        xw = sb.tile([P, S], U32, align_bytes=64)
        for j0 in range(0, S, HALF):
            nc.vector.tensor_copy(xw[:, j0 : j0 + HALF], xw_win[:].indirect(entries(offs_t, j0, HALF)))

        ident = sb.tile([P, P], F32)
        make_identity(nc, ident[:])

        s_ps = [ps.tile([P, S], F32, name="s_ps%d" % t, tag="bank%d" % t) for t in range(PACK)]
        for pair in range(0, PACK, 2):
            for j0 in range(0, S, HALF):
                for t in (pair, pair + 1):
                    nc.tensor.matmul_mx(
                        out=s_ps[t][:, j0 : j0 + HALF],
                        lhsT=dw[:, t, :].bitcast(FP8X4),
                        lhsT_scale=planes[:, t * P : (t + 1) * P],
                        rhs=xw[:, j0 : j0 + HALF].bitcast(FP8X4),
                        rhs_scale=planes[:, H + j0 : H + j0 + HALF],
                        start=True,
                        stop=True,
                    )
        a_t = []
        for t in range(PACK):
            a = sb.tile([P, 2 * S], F32, name="a%d" % t)
            if t == 0:
                nc.scalar.activation(a[:, 0:S], s_ps[t][:], ACT.Exp, scale=HALF_SCORE)
            elif t < PACK - 1:
                nc.scalar.activation(a[:, 0:S], s_ps[t][:], ACT.Copy, scale=HALF_SCORE)
            else:
                nc.vector.tensor_scalar(a[:, 0:S], s_ps[t][:], HALF_SCORE, None, ALU.mult)
            a_t.append(a)

        tab_t = [tab0]
        for t in range(1, PACK):
            tile = sb.tile([P, 2 * J], F32, name="tab%d" % t, align_bytes=64, tag="late%d" % (t - 1))
            nc.sync.dma_start(tile[:, 0:J], tab_rows[:, t, :])
            tab_t.append(tile)
        w_raw = sb.tile([P, PACK, N], F32, align_bytes=64, tag="late4")
        w_rows = w1.rearrange("(b j r) c -> j b r c", j=PACK, r=RUN)
        for j in range(PACK):
            nc.sync.dma_start(w_raw[:, j, :], w_rows[j])
        gn_t = sb.tile([P, PACK, 8], F32, align_bytes=64, tag="late5")
        with nc.allow_non_contiguous_dma(reason="one weight a key"):
            for t in range(PACK):
                nc.sync.dma_start(gn_t[:, t, 0:1], gn.rearrange("(b t r) o -> t b r o", t=PACK, r=RUN)[t])

        e1 = sb.tile([P, PACK, S], F32)
        e2 = sb.tile([P, PACK, S], F32)
        u0 = sb.tile([P, S], F32, align_bytes=64)
        nc.vector.tensor_copy(e1[:, 0, :], a_t[0][:].indirect(n1_t[:]))
        nc.vector.tensor_tensor(u0[:], a_t[0][:].indirect(n2_t[:]), e1[:, 0, :], ALU.add)
        ut_ps = [ps.tile([P, PACK - 1, P], F32, name="ut_ps%d" % q, tag="bank%d" % (PACK + q)) for q in range(S // QUART)]
        for t in range(1, PACK):
            for lst, e in ((n1_t, e1), (n2_t, e2)):
                nc.scalar.activation(e[:, t, :], a_t[t][:].indirect(lst[:]), ACT.Exp)
                for q in range(S // QUART):
                    nc.tensor.matmul(
                        ut_ps[q][:, t - 1, :],
                        e[:, t, q * QUART : (q + 1) * QUART],
                        ident[:],
                        start=(t == 1 and lst is n1_t),
                        stop=(t == PACK - 1 and lst is n2_t),
                        is_transpose=True,
                    )

        lg0 = sb.tile([P, S], F32, align_bytes=64)
        df = sb.tile([P, PACK, S], F32)
        nc.scalar.activation(lg0[:], u0[:], ACT.Ln)
        nc.vector.scalar_tensor_tensor(df[:, 0, :], s_ps[0][:], HALF_SCORE, lg0[:], ALU.mult, ALU.subtract)
        lgt = sb.tile([P, S // QUART, PACK - 1, P], F32, tag="lgt", align_bytes=64)
        for hf in range(2):
            for q in (2 * hf, 2 * hf + 1):
                nc.scalar.activation(lgt[:, q, :, :], ut_ps[q][:], ACT.Ln)
            for t in range(1, PACK):
                lg_ps = ps.tile([P, HALF], F32, name="lg_ps%d_%d" % (hf, t), tag="bank%d" % ((PACK - 1) * hf + t))
                for q in range(2):
                    nc.tensor.transpose(lg_ps[:, q * QUART : (q + 1) * QUART], lgt[:, 2 * hf + q, t - 1, :], ident[:])
                cols = slice(hf * HALF, (hf + 1) * HALF)
                nc.vector.tensor_tensor(df[:, t, cols], a_t[t][:, cols], lg_ps[:], ALU.subtract)

        w_bf = sb.tile([P, PACK, P, PACK], BF16, align_bytes=64)
        nc.gpsimd.tensor_scalar(
            w_bf[:].rearrange("p t m j -> p m t j"),
            w_raw[:].rearrange("p j (m t) -> p m t j", t=PACK),
            1.0,
            0.0,
            ALU.mult,
            ALU.add,
        )
        w_codes = sb.tile([P, N], U32, align_bytes=64)
        w_sc = sb.tile([P, N], U8, align_bytes=64)
        nc.vector.quantize_mx(out=w_codes[:].bitcast(FP8X4), scales=w_sc[:], in_=w_bf[:].rearrange("p t m j -> p (t m j)"))
        gn2 = sb.tile([P, PACK], F32)
        nc.vector.tensor_scalar(gn2[:], gn_t[:, :, 0], 2.0, None, ALU.mult)

        h_t = [sb.tile([P, 2 * S], F32, name="h%d" % t) for t in range(PACK)]
        h_ps = [ps.tile([P, S], F32, name="h_ps%d" % t, tag="bank%d" % t) for t in range(PACK)]
        sg = sb.tile([P, PACK, S], F32)
        z_codes = sb.tile([P, S], U32, align_bytes=64)
        z_sc = sb.tile([P, S], U8, align_bytes=64)

        def weigh(z_bf, j0, lo, wd):
            cols = slice(j0 + lo, j0 + lo + wd)
            nc.scalar.activation(sg[:, :, cols], df[:, :, cols], ACT.Sigmoid)
            nc.vector.tensor_tensor(
                z_bf[:, lo : lo + wd, :].rearrange("p (c i) t -> p c t i", i=4),
                sg[:, :, cols].rearrange("p t (c i) -> p c t i", i=4),
                gn2[:].unsqueeze(1).unsqueeze(3).to_broadcast([P, wd // 4, PACK, 4]),
                ALU.mult,
            )

        def quantise(z_bf, j0, wd):
            nc.vector.quantize_mx(
                out=z_codes[:, j0 : j0 + wd].bitcast(FP8X4),
                scales=z_sc[:, j0 : j0 + wd],
                in_=z_bf[:].rearrange("p j t -> p (j t)"),
            )

        pending = None
        for j0, wd in Z_PIECES:
            z_bf = sb.tile([P, wd, PACK], BF16, name="z_bf%d" % j0, tag="z_bf%d" % j0, align_bytes=64)
            step = FIRST_STEP if j0 == 0 else wd
            for lo in range(0, wd, step):
                weigh(z_bf, j0, lo, step)
            if pending is not None:
                quantise(*pending)
            pending = (z_bf, j0, wd)
        quantise(*pending)

        for j0 in range(0, S, HALF):
            for t in range(PACK):
                nc.tensor.matmul_mx(
                    out=h_ps[t][:, j0 : j0 + HALF],
                    lhsT=w_codes[:, t * P : (t + 1) * P].bitcast(FP8X4),
                    lhsT_scale=w_sc[:, t * P : (t + 1) * P],
                    rhs=z_codes[:, j0 : j0 + HALF].bitcast(FP8X4),
                    rhs_scale=z_sc[:, j0 : j0 + HALF],
                    start=True,
                    stop=True,
                )
                nc.scalar.copy(h_t[t][:, j0 : j0 + HALF], h_ps[t][:, j0 : j0 + HALF])

        g3 = []
        g4 = []
        for t in range(PACK):
            g3.append(sb.tile([P, S], F32, name="g3_%d" % t))
            nc.vector.tensor_copy(g3[t][:], tab_t[t][:].indirect(n3_t[:]))
            if t < PACK - 1:
                g4.append(sb.tile([P, S], F32, name="g4_%d" % t))
                nc.vector.tensor_copy(g4[t][:], tab_t[t][:].indirect(n4_t[:]))
        g4_last = []
        for j0, tag in ((0, "lgt"), (HALF, "z_bf%d" % Z_PIECES[-1][0])):
            tile = sb.tile([P, HALF], F32, name="g4_last%d" % j0, tag=tag, align_bytes=64)
            nc.vector.tensor_copy(tile[:], tab_t[PACK - 1][:].indirect(entries(n4_t, j0, HALF)))
            g4_last.append(tile)

        out_rows = out.rearrange("(p t) j -> p t j", t=PACK)
        y = sb.tile([P, PACK, S], F32)
        res = sb.tile([P, PACK, S], F32)
        for t in range(PACK):
            step = HALF if t == PACK - 1 else S
            for j0 in range(0, S, step):
                nc.vector.tensor_tensor(
                    y[:, t, j0 : j0 + step],
                    h_t[t][:].indirect(entries(n5_t, j0, step)),
                    g3[t][:, j0 : j0 + step],
                    ALU.mult,
                )
            if t == 0:
                sum_ps = ps.tile([P, S // QUART, P], F32, name="sum_ps0", tag="bank4")
                for first, src in ((True, g4[t][:]), (False, y[:, t, :])):
                    for q in range(S // QUART):
                        nc.tensor.matmul(
                            sum_ps[:, q, :],
                            src[:, q * QUART : (q + 1) * QUART],
                            ident[:],
                            start=(first and q == 0),
                            stop=(not first and q == S // QUART - 1),
                            is_transpose=True,
                        )
                sum_t = sb.tile([P, S // QUART, P], F32, name="sum_t0")
                nc.scalar.copy(sum_t[:], sum_ps[:])
                back_ps = ps.tile([P, S], F32, name="back_ps0", tag="bank5")
                for q in range(S // QUART):
                    nc.tensor.transpose(back_ps[:, q * QUART : (q + 1) * QUART], sum_t[:, q, :], ident[:])
                nc.scalar.copy(res[:, t, :], back_ps[:])
                nc.scalar.dma_start(out_rows[:, t, :], res[:, t, :])
            elif t < PACK - 1:
                nc.vector.tensor_tensor(res[:, t, :], y[:, t, :], g4[t][:], ALU.add)
                nc.sync.dma_start(out_rows[:, t, :], res[:, t, :])
            else:
                for hf in range(2):
                    cols = slice(hf * HALF, (hf + 1) * HALF)
                    nc.vector.tensor_tensor(res[:, t, cols], y[:, t, cols], g4_last[hf][:], ALU.add)
                    nc.sync.dma_start(out_rows[:, t, cols], res[:, t, cols])
